import numpy as np
import ml_dtypes


def mxq(x, axis, fmt="e4m3"):
    dtype, down = {"e4m3": (ml_dtypes.float8_e4m3fn, 7), "e5m2": (ml_dtypes.float8_e5m2, 14)}[fmt]
    v = np.moveaxis(np.asarray(x, np.float32).astype(ml_dtypes.bfloat16).astype(np.float64), axis, -1)
    blocks = v.reshape(v.shape[:-1] + (-1, 32))
    amax = np.abs(blocks).max(-1, keepdims=True)
    byte = np.maximum(np.where(amax > 0, np.frexp(amax)[1] - 1 + 127, 0) - down, 1)
    scale = np.exp2(byte - 127.0)
    codes = (blocks / scale).astype(np.float32).astype(dtype).astype(np.float64)
    return np.moveaxis((codes * scale).reshape(v.shape), -1, axis)


WIDE = False


def mx_kscale(k):
    if not WIDE:
        return np.ones(k)
    levels = np.array([10, -10, 5, -5, 0])
    if k % 512:
        return np.exp2(np.random.permutation(np.resize(levels, k // 32))).repeat(32)
    a = np.empty((k // 512, 16))
    for p in range(k // 512):
        a[p, :8] = np.random.permutation(np.resize(levels, 8))
        for g in range(8):
            far = levels[np.abs(levels - a[p, g]) >= 10]
            a[p, g + 8] = far[np.random.randint(len(far))]
    return np.exp2(a.ravel()).repeat(32)


def f64(x):
    return np.asarray(x).astype(np.float64)


def striped(idx):
    return np.tile(idx.reshape(-1, 16).T, (8, 1)).astype(np.uint16)


def unstriped(offs):
    return offs[:16].T.reshape(-1).astype(np.int64)


def pack_weight(w):
    k, n = w.shape
    w = f64(np.asarray(w, np.float32).astype(ml_dtypes.bfloat16)).reshape(k // 32, 32, n)
    amax = np.abs(w).max(1)
    byte = np.clip(np.where(amax > 0, np.frexp(amax)[1] - 1 + 127 - 7, 1), 1, 254)
    scaled = (w * np.exp2(127.0 - byte)[:, None, :]).reshape(k, n).astype(np.float32)
    words = np.ascontiguousarray(scaled.reshape(k // 512, 128, 4, n).transpose(0, 1, 3, 2)).astype(ml_dtypes.float8_e4m3fn).view(np.uint8)
    return words, np.ascontiguousarray(byte.astype(np.uint8).reshape(k // 512, 16, n))


def unpack_weight(words, scales):
    g, p, n, _ = words.shape
    vals = np.ascontiguousarray(words).view(ml_dtypes.float8_e4m3fn).astype(np.float64) * np.repeat(np.exp2(scales.astype(np.float64) - 127.0), 8, axis=1)[..., None]
    return vals.transpose(0, 1, 3, 2).reshape(g * 512, n)


E2M1 = np.array([0.0, 0.5, 1.0, 1.5, 2.0, 3.0, 4.0, 6.0, -0.0, -0.5, -1.0, -1.5, -2.0, -3.0, -4.0, -6.0])


def pack_fp4(w):
    k, n = w.shape
    w = f64(np.asarray(w, np.float32).astype(ml_dtypes.bfloat16)).reshape(k // 32, 32, n)
    amax = np.abs(w).max(1)
    mant, ex = np.frexp(amax / 6.0)
    byte = np.clip(np.where(amax > 0, np.where(mant > 0.5, ex, ex - 1) + 127, 1), 1, 254)
    scaled = (w * np.exp2(127.0 - byte)[:, None, :]).reshape(k, n).astype(np.float32)
    c = np.ascontiguousarray(scaled.reshape(k // 512, 128, 4, n).transpose(0, 1, 3, 2)).astype(ml_dtypes.float4_e2m1fn).view(np.uint8) & 0xF
    words = (c[..., 0::2] | (c[..., 1::2] << 4)).reshape(k // 512, 128, 2 * n)
    return np.ascontiguousarray(words), np.ascontiguousarray(byte.astype(np.uint8).reshape(k // 512, 16, n))


def unpack_fp4(words, scales):
    g, _, n = scales.shape
    words = np.ascontiguousarray(words).reshape(g, 128, n, 2)
    nib = np.empty((g, 128, n, 4), np.uint8)
    nib[..., 0::2] = words & 0xF
    nib[..., 1::2] = words >> 4
    vals = E2M1[nib] * np.repeat(np.exp2(scales.astype(np.float64) - 127.0), 8, axis=1)[..., None]
    return vals.transpose(0, 1, 3, 2).reshape(g * 512, n)


K, T, S, D, N, H = 1024, 2048, 512, 4, 256, 512


def setup_inputs():
    n = np.random.standard_normal
    s = mx_kscale(K)[:, None]
    u = mx_kscale(H)
    packed_xT = pack_weight(n((K, T)) * s)
    packed_w1 = pack_fp4(n((K, H)) / np.sqrt(K) / s)
    packed_w2 = pack_fp4(n((K, H)) / np.sqrt(K) / s)
    packed_w3 = pack_fp4(n((H, N)) / np.sqrt(H) / u[:, None])
    return {
        "x_words": packed_xT[0],
        "x_scales": packed_xT[1],
        "w1_words": packed_w1[0],
        "w1_scales": packed_w1[1],
        "w2_words": packed_w2[0],
        "w2_scales": packed_w2[1],
        "nu": (0.7 * n((H, S))).astype(np.float32),
        "obs": (np.random.uniform(0.1, 0.4, (H, S))).astype(np.float32),
        "unit": (np.random.uniform(0.6, 1.4, (H, 1)) * u[:, None]).astype(np.float32),
        "w3_words": packed_w3[0],
        "w3_scales": packed_w3[1],
        "offs": striped(np.random.permutation(T)[:S]),
        "riv": striped(np.random.permutation(S)),
    }


def reference(x_words, x_scales, w1_words, w1_scales, w2_words, w2_scales, nu, obs, unit, w3_words, w3_scales, offs, riv):
    xq = unpack_weight(x_words, x_scales)[:, unstriped(offs)]
    dl = unpack_fp4(w1_words, w1_scales).T @ xq
    mu = unpack_fp4(w2_words, w2_scales).T @ xq
    util = np.tanh(dl) + np.tanh(mu) * f64(nu)
    eu = np.exp(0.9 * util)
    mkt = eu.reshape(len(eu), -1, D).sum(axis=2)
    shr = eu / (np.repeat(mkt, D, axis=1) + 1.0)
    dnew = dl + np.log(f64(obs)) - np.log(shr)
    crs = shr * shr[:, unstriped(riv)]
    hid = f64(unit) * (dnew * (-1.0 * shr + 1.0) - crs)
    return unpack_fp4(w3_words, w3_scales).T @ mxq(hid, 0, "e4m3")

@@ -1,0 +1,236 @@
+from contextlib import ExitStack
+
+import concourse.mybir as mybir
+
+K, T, S, D, N, H = 1024, 2048, 512, 4, 256, 512
+FLOPS = 2 * (2 * K * H * S + H * N * S)
+
+F32 = mybir.dt.float32
+BF16 = mybir.dt.bfloat16
+I32 = mybir.dt.int32
+U32 = mybir.dt.uint32
+U16 = mybir.dt.uint16
+U8 = mybir.dt.uint8
+FP8X4 = mybir.dt.float8_e4m3fn_x4
+FP4X4 = mybir.dt.float4_e2m1fn_x4
+ALU = mybir.AluOpType
+ACT = mybir.ActivationFunctionType
+AX = mybir.AxisListType
+
+P = 128
+PACK = 4
+PASSES = K // (P * PACK)
+V = S // D
+HALF = S // 2
+
+
+def tile_picked_yblpsh_crs_p_kernel(
+    tc, x_words, x_scales, w1_words, w1_scales, w2_words, w2_scales, nu, obs, unit, w3_words, w3_scales, offs, riv, out
+):
+    nc = tc.nc
+    with ExitStack() as ctx:
+        keep = ctx.enter_context(tc.tile_pool(name="keep", bufs=1))
+        psum = ctx.enter_context(tc.psum_pool(name="psum", bufs=1))
+
+        def tiles(name, shape, dtype, count):
+            return [keep.tile(shape, dtype, name=name + str(i), align_bytes=64) for i in range(count)]
+
+        def load_plane_rows(queue, plane, scales, quadrant):
+            queue.dma_start(
+                out=plane[32 * quadrant : 32 * quadrant + 4].bitcast(I32),
+                in_=scales[:, 4 * quadrant : 4 * quadrant + 4, :].rearrange("o r c -> r o c").bitcast(I32),
+            )
+
+        offs_t = keep.tile([P, S // 16], U16, name="offs_t")
+        riv_t = keep.tile([P, S // 16], U16, name="riv_t")
+        xs = keep.tile([P, PASSES, T], U8, name="xs", tag="xs_then_nu", align_bytes=64)
+        ws = tiles("ws", [P, PASSES, H], U8, 2)
+        w3s = keep.tile([P, 1, N], U8, name="w3s", align_bytes=64)
+        ww = keep.tile([P, 2 * PASSES, 2 * H], U8, name="ww", align_bytes=64)
+        w3w = keep.tile([P, 2 * N], U8, name="w3w", align_bytes=64)
+        xw = [keep.tile([P, T], I32, name="xw%d" % o, tag="xw%d" % o, align_bytes=64) for o in range(PASSES)]
+        unit_t = keep.tile([P, PACK], F32, name="unit_t")
+
+        nc.vector.memset(xs[:].bitcast(I32), 0)
+        nc.gpsimd.memset(ws[1][:].bitcast(I32), 0)
+        nc.gpsimd.memset(ws[0][:].bitcast(I32), 0)
+
+        nc.sync.dma_start(offs_t[:], offs)
+        nc.sync.dma_start(riv_t[:], riv)
+        for w, words in enumerate((w1_words, w2_words)):
+            nc.sync.dma_start(
+                out=ww[:, PASSES * w : PASSES * (w + 1), :].bitcast(I32), in_=words.rearrange("o p c -> p o c").bitcast(I32)
+            )
+        for o in range(PASSES):
+            nc.sync.dma_start(out=xw[o][:], in_=x_words[o].rearrange("p c r -> p (c r)").bitcast(I32))
+        for q in range(4):
+            load_plane_rows(nc.scalar, xs, x_scales, q)
+        for q in range(4):
+            load_plane_rows(nc.gpsimd, ws[1], w2_scales, q)
+        for q in range(4):
+            load_plane_rows(nc.scalar if q < 3 else nc.gpsimd, ws[0], w1_scales, q)
+        nc.gpsimd.memset(w3s[:].bitcast(I32), 0)
+        nc.gpsimd.dma_start(out=unit_t[:], in_=unit.rearrange("(p t) o -> p (t o)", t=PACK))
+        nc.gpsimd.dma_start(out=w3w[:].bitcast(I32), in_=w3_words[0].bitcast(I32))
+        for q in range(4):
+            load_plane_rows(nc.gpsimd, w3s, w3_scales, q)
+
+        wd = tiles("wd", [P, 2 * PASSES, 2 * P], U8, PACK)
+        wsd = [tiles("wsd%d_" % w, [P, PASSES, P], U8, PACK) for w in range(2)]
+
+        def deal(t):
+            nc.vector.tensor_copy(
+                out=wd[t][:].rearrange("p a (m b) -> p a m b", b=2),
+                in_=ww[:].rearrange("p a (m t b) -> p a m t b", t=PACK, b=2)[:, :, :, t, :],
+            )
+            for w in range(2):
+                nc.vector.tensor_copy(out=wsd[w][t][:], in_=ws[w][:].rearrange("p o (m t) -> p o m t", t=PACK)[:, :, :, t])
+
+        xg = tiles("xg", [P, S], U32, PASSES)
+        sg = tiles("sg", [P, S], U8, PASSES)
+        for o in range(PASSES):
+            nc.vector.tensor_copy(out=sg[o][:], in_=xs[:, o, :].indirect(offs_t[:]))
+        for o in range(PASSES):
+            nc.vector.tensor_copy(out=xg[o][:], in_=xw[o][:].bitcast(U32).indirect(offs_t[:]))
+        deal(0)
+        for t in range(1, PACK):
+            deal(t)
+        nu_t = keep.tile([P, PACK, S], F32, name="nu_t", tag="xs_then_nu", align_bytes=64)
+        obs_t = keep.tile([P, PACK, S], F32, name="obs_t", tag="xw0", align_bytes=64)
+        nu_rows = nu.rearrange("(p t) j -> p t j", t=PACK)
+        for h in range(2):
+            nc.sync.dma_start(out=nu_t[:, 2 * h : 2 * h + 2, :], in_=nu_rows[:, 2 * h : 2 * h + 2, :])
+        nc.sync.dma_start(out=obs_t[:], in_=obs.rearrange("(p t) j -> p t j", t=PACK))
+
+        dl = [psum.tile([P, S], F32, name="dl%d" % t) for t in range(PACK)]
+        mu = [psum.tile([P, S], F32, name="mu%d" % t, tag="bank%d" % t) for t in range(PACK)]
+
+        def first_products(t, o):
+            for w, acc in ((1, mu[t]), (0, dl[t])):
+                nc.tensor.matmul_mx(
+                    out=acc[:],
+                    lhsT=wd[t][:, PASSES * w + o, :].bitcast(FP4X4),
+                    lhsT_scale=wsd[w][t][:, o, :],
+                    rhs=xg[o][:].bitcast(FP8X4),
+                    rhs_scale=sg[o][:],
+                    start=(o == 0),
+                    stop=(o == PASSES - 1),
+                )
+
+        for o in range(PASSES):
+            for t in range(PACK):
+                first_products(t, o)
+
+        tm = tiles("tm", [P, S], F32, PACK)
+        td = tiles("td", [P, S], F32, PACK)
+        taste = tiles("taste", [P, S], F32, PACK)
+        util = tiles("util", [P, S], F32, PACK)
+        eu = keep.tile([P, PACK, S], F32, name="eu", tag="eu_then_lnobs")
+        mkt = keep.tile([P, PACK, V], F32, name="mkt")
+
+        def utility(t):
+            nc.scalar.activation(out=tm[t][:], in_=mu[t][:], func=ACT.Tanh)
+            nc.scalar.activation(out=td[t][:], in_=dl[t][:], func=ACT.Tanh)
+            nc.vector.tensor_tensor(out=taste[t][:], in0=tm[t][:], in1=nu_t[:, t, :], op=ALU.mult)
+            nc.vector.tensor_tensor(out=util[t][:], in0=taste[t][:], in1=td[t][:], op=ALU.add)
+
+        def market(t):
+            nc.scalar.activation(out=eu[:, t, :], in_=util[t][:], func=ACT.Exp, scale=0.9)
+            nc.vector.tensor_reduce(out=mkt[:, t, :], in_=eu[:, t, :].rearrange("p (v d) -> p v d", d=D), axis=AX.X, op=ALU.add)
+
+        utility(0)
+        for t in range(1, PACK):
+            utility(t)
+            market(t - 1)
+        market(PACK - 1)
+
+        lnden = keep.tile([P, PACK, V], F32, name="lnden")
+        lnobs = keep.tile([P, PACK, S], F32, name="lnobs", tag="eu_then_lnobs")
+        nc.scalar.activation(out=lnden[:], in_=mkt[:], func=ACT.Ln, bias=1.0)
+        for h in range(2):
+            nc.scalar.activation(out=lnobs[:, 2 * h : 2 * h + 2, :], in_=obs_t[:, 2 * h : 2 * h + 2, :], func=ACT.Ln)
+
+        lnshr = tiles("lnshr", [P, S], F32, PACK)
+        gap = tiles("gap", [P, S], F32, PACK)
+        dnew = tiles("dnew", [P, S], F32, PACK)
+        shr = tiles("shr", [P, S], F32, PACK)
+        rival = tiles("rival", [P, S], F32, PACK)
+        both = tiles("both", [P, S], F32, PACK)
+        cut = tiles("cut", [P, S], F32, PACK)
+        hid = tiles("hid", [P, PACK, HALF], BF16, 2)
+
+        def log_share(t):
+            nc.vector.scalar_tensor_tensor(
+                out=lnshr[t][:].rearrange("p (v d) -> p v d", d=D),
+                in0=util[t][:].rearrange("p (v d) -> p v d", d=D),
+                scalar=0.9,
+                in1=lnden[:, t, :].unsqueeze(2).to_broadcast([P, V, D]),
+                op0=ALU.mult,
+                op1=ALU.subtract,
+            )
+
+        def minus_log_share(t):
+            nc.vector.tensor_tensor(out=gap[t][:], in0=dl[t][:], in1=lnshr[t][:], op=ALU.subtract)
+
+        log_share(0)
+        for t in range(1, PACK):
+            log_share(t)
+            minus_log_share(t - 1)
+        minus_log_share(PACK - 1)
+        for t in range(PACK):
+            nc.vector.tensor_tensor(out=dnew[t][:], in0=gap[t][:], in1=lnobs[:, t, :], op=ALU.add)
+        for t in range(PACK):
+            nc.scalar.activation(out=shr[t][:], in_=lnshr[t][:], func=ACT.Exp)
+            for h in range(2):
+                nc.scalar.activation(
+                    out=rival[t][:, h * HALF : (h + 1) * HALF],
+                    in_=shr[t][:].indirect(riv_t[:, h * (HALF // 16) : (h + 1) * (HALF // 16)]),
+                    func=ACT.Copy,
+                )
+
+        def step(kind, t, h):
+            cols = slice(h * HALF, (h + 1) * HALF)
+            u = unit_t[:, t : t + 1]
+            if kind == 0:
+                nc.vector.tensor_tensor(out=both[t][:, cols], in0=rival[t][:, cols], in1=dnew[t][:, cols], op=ALU.add)
+            elif kind == 1:
+                nc.vector.scalar_tensor_tensor(
+                    out=cut[t][:, cols], in0=both[t][:, cols], scalar=u, in1=shr[t][:, cols], op0=ALU.mult, op1=ALU.mult
+                )
+            else:
+                nc.vector.scalar_tensor_tensor(
+                    out=hid[h][:, t, :], in0=dnew[t][:, cols], scalar=u, in1=cut[t][:, cols], op0=ALU.mult, op1=ALU.subtract
+                )
+
+        for t in range(PACK):
+            for kind in range(3):
+                for h in range(2):
+                    step(kind, t, h)
+
+        woven = tiles("woven", [P, HALF, PACK], BF16, 2)
+        codes = tiles("codes", [P, HALF], U32, 2)
+        plane = tiles("plane", [P, HALF], U8, 2)
+        res = tiles("res", [P, HALF], F32, 4)
+        for h in range(2):
+            nc.vector.tensor_copy(
+                out=woven[h][:].rearrange("p (c i) t -> p c t i", i=4), in_=hid[h][:].rearrange("p t (c i) -> p c t i", i=4)
+            )
+        for h in range(2):
+            nc.vector.quantize_mx(out=codes[h][:].bitcast(FP8X4), scales=plane[h][:], in_=woven[h][:].rearrange("p j t -> p (j t)"))
+        for h in range(2):
+            for m in range(N // P):
+                acc = psum.tile([P, HALF], F32, name="acc%d%d" % (h, m), tag="bank%d" % (2 * h + m))
+                nc.tensor.matmul_mx(
+                    out=acc[:],
+                    lhsT=w3w[:, 2 * P * m : 2 * P * (m + 1)].bitcast(FP4X4),
+                    lhsT_scale=w3s[:, 0, P * m : P * (m + 1)],
+                    rhs=codes[h][:].bitcast(FP8X4),
+                    rhs_scale=plane[h][:],
+                    start=True,
+                    stop=True,
+                )
+                if m == 0:
+                    nc.scalar.copy(out=res[2 * h + m][:], in_=acc[:])
+                else:
+                    nc.vector.tensor_copy(out=res[2 * h + m][:], in_=acc[:])
+                nc.sync.dma_start(out=out[P * m : P * (m + 1), h * HALF : (h + 1) * HALF], in_=res[2 * h + m][:])

@@ -33,7 +33,7 @@ def tile_picked_yblpsh_crs_p_kernel(
         psum = ctx.enter_context(tc.psum_pool(name="psum", bufs=1))
 
         def tiles(name, shape, dtype, count):
-            return [keep.tile(shape, dtype, name=name + str(i), align_bytes=64) for i in range(count)]
+            return [keep.tile(shape, dtype, name=name + str(i), tag=name + str(i), align_bytes=64) for i in range(count)]
 
         def load_plane_rows(queue, plane, scales, quadrant):
             queue.dma_start(
@@ -45,72 +45,90 @@ def tile_picked_yblpsh_crs_p_kernel(
         riv_t = keep.tile([P, S // 16], U16, name="riv_t")
         xs = keep.tile([P, PASSES, T], U8, name="xs", tag="xs_then_nu", align_bytes=64)
         ws = tiles("ws", [P, PASSES, H], U8, 2)
-        w3s = keep.tile([P, 1, N], U8, name="w3s", align_bytes=64)
-        ww = keep.tile([P, 2 * PASSES, 2 * H], U8, name="ww", align_bytes=64)
-        w3w = keep.tile([P, 2 * N], U8, name="w3w", align_bytes=64)
+        ww = keep.tile([P, 2 * PASSES, 2 * H], U8, name="ww", tag="ww", align_bytes=64)
         xw = [keep.tile([P, T], I32, name="xw%d" % o, tag="xw%d" % o, align_bytes=64) for o in range(PASSES)]
+
+        nu_t = keep.tile([P, PACK, S], F32, name="nu_t")
+        w3s = keep.tile([P, 1, N], U8, name="w3s", align_bytes=64)
+        w3w = keep.tile([P, 2 * N], U8, name="w3w", align_bytes=64)
         unit_t = keep.tile([P, PACK], F32, name="unit_t")
+        xs_words = xs[:].rearrange("p o c -> p (o c)").bitcast(I32)
+        nc.gpsimd.memset(xs_words[:, 0:640], 0)
+        nc.vector.memset(xs_words[:, 640:1024], 0)
+        nc.vector.memset(ws[0][:].bitcast(I32), 0)
+        nc.vector.memset(ws[1][:].bitcast(I32), 0)
 
-        nc.vector.memset(xs[:].bitcast(I32), 0)
-        nc.gpsimd.memset(ws[1][:].bitcast(I32), 0)
-        nc.gpsimd.memset(ws[0][:].bitcast(I32), 0)
-
+        nc.vector.memset(w3s[:].bitcast(I32), 0)
+        obs_t = keep.tile([P, PACK, S], F32, name="obs_t", align_bytes=64)
         nc.sync.dma_start(offs_t[:], offs)
-        nc.sync.dma_start(riv_t[:], riv)
         for w, words in enumerate((w1_words, w2_words)):
             nc.sync.dma_start(
                 out=ww[:, PASSES * w : PASSES * (w + 1), :].bitcast(I32), in_=words.rearrange("o p c -> p o c").bitcast(I32)
             )
-        for o in range(PASSES):
-            nc.sync.dma_start(out=xw[o][:], in_=x_words[o].rearrange("p c r -> p (c r)").bitcast(I32))
         for q in range(4):
-            load_plane_rows(nc.scalar, xs, x_scales, q)
+            load_plane_rows(nc.sync, xs, x_scales, q)
+        nc.sync.dma_start(out=xw[0][:], in_=x_words[0].rearrange("p c r -> p (c r)").bitcast(I32))
         for q in range(4):
-            load_plane_rows(nc.gpsimd, ws[1], w2_scales, q)
+            load_plane_rows(nc.sync, ws[0], w1_scales, q)
         for q in range(4):
-            load_plane_rows(nc.scalar if q < 3 else nc.gpsimd, ws[0], w1_scales, q)
-        nc.gpsimd.memset(w3s[:].bitcast(I32), 0)
+            load_plane_rows(nc.sync if q < 1 else nc.gpsimd, ws[1], w2_scales, q)
         nc.gpsimd.dma_start(out=unit_t[:], in_=unit.rearrange("(p t) o -> p (t o)", t=PACK))
-        nc.gpsimd.dma_start(out=w3w[:].bitcast(I32), in_=w3_words[0].bitcast(I32))
-        for q in range(4):
-            load_plane_rows(nc.gpsimd, w3s, w3_scales, q)
-
-        wd = tiles("wd", [P, 2 * PASSES, 2 * P], U8, PACK)
-        wsd = [tiles("wsd%d_" % w, [P, PASSES, P], U8, PACK) for w in range(2)]
-
-        def deal(t):
-            nc.vector.tensor_copy(
-                out=wd[t][:].rearrange("p a (m b) -> p a m b", b=2),
-                in_=ww[:].rearrange("p a (m t b) -> p a m t b", t=PACK, b=2)[:, :, :, t, :],
-            )
-            for w in range(2):
-                nc.vector.tensor_copy(out=wsd[w][t][:], in_=ws[w][:].rearrange("p o (m t) -> p o m t", t=PACK)[:, :, :, t])
-
-        xg = tiles("xg", [P, S], U32, PASSES)
-        sg = tiles("sg", [P, S], U8, PASSES)
-        for o in range(PASSES):
-            nc.vector.tensor_copy(out=sg[o][:], in_=xs[:, o, :].indirect(offs_t[:]))
-        for o in range(PASSES):
-            nc.vector.tensor_copy(out=xg[o][:], in_=xw[o][:].bitcast(U32).indirect(offs_t[:]))
-        deal(0)
-        for t in range(1, PACK):
-            deal(t)
-        nu_t = keep.tile([P, PACK, S], F32, name="nu_t", tag="xs_then_nu", align_bytes=64)
-        obs_t = keep.tile([P, PACK, S], F32, name="obs_t", tag="xw0", align_bytes=64)
+        obs_rows = obs.rearrange("(p t) j -> p t j", t=PACK)
+        for h in range(2):
+            nc.sync.dma_start(out=obs_t[:, 2 * h : 2 * h + 2, :], in_=obs_rows[:, 2 * h : 2 * h + 2, :])
+        nc.sync.dma_start(out=xw[1][:], in_=x_words[1].rearrange("p c r -> p (c r)").bitcast(I32))
         nu_rows = nu.rearrange("(p t) j -> p t j", t=PACK)
         for h in range(2):
             nc.sync.dma_start(out=nu_t[:, 2 * h : 2 * h + 2, :], in_=nu_rows[:, 2 * h : 2 * h + 2, :])
-        nc.sync.dma_start(out=obs_t[:], in_=obs.rearrange("(p t) j -> p t j", t=PACK))
+        nc.sync.dma_start(riv_t[:], riv)
+        nc.sync.dma_start(out=w3w[:].bitcast(I32), in_=w3_words[0].bitcast(I32))
+        for q in range(4):
+            load_plane_rows(nc.sync, w3s, w3_scales, q)
 
-        dl = [psum.tile([P, S], F32, name="dl%d" % t) for t in range(PACK)]
+        lnobs = keep.tile([P, PACK, S], F32, name="lnobs")
+        for h in range(2):
+            nc.scalar.activation(out=lnobs[:, 2 * h : 2 * h + 2, :], in_=obs_t[:, 2 * h : 2 * h + 2, :], func=ACT.Ln)
+
+        wd = [
+            keep.tile([P, 2 * PASSES, 2, 2 * P], U8, name="wd%d" % h, tag=tag, align_bytes=64) for h, tag in enumerate(("wd0", "xw1"))
+        ]
+        wsd = tiles("wsd", [P, PASSES, H], U8, 2)
+
+        def deal_words(t):
+            nc.vector.tensor_copy(
+                out=wd[t // 2][:, :, t % 2, :].rearrange("p a (m b) -> p a m b", b=2),
+                in_=ww[:].rearrange("p a (m t b) -> p a m t b", t=PACK, b=2)[:, :, :, t, :],
+            )
+
+        def deal_scales(w):
+            nc.vector.tensor_copy(
+                out=wsd[w][:].rearrange("p o (t m) -> p o t m", t=PACK), in_=ws[w][:].rearrange("p o (m t) -> p o t m", t=PACK)
+            )
+
+        xg = [keep.tile([P, S], U32, name="xg%d" % o, tag=tag, align_bytes=64) for o, tag in enumerate(("xg0", "ws1"))]
+        sg = tiles("sg", [P, S], U8, PASSES)
+        deal_words(0)
+        deal_words(1)
+        nc.vector.tensor_copy(out=sg[0][:], in_=xs[:, 0, :].indirect(offs_t[:]))
+        nc.vector.tensor_copy(out=xg[0][:], in_=xw[0][:].bitcast(U32).indirect(offs_t[:]))
+        deal_scales(0)
+        deal_scales(1)
+        nc.vector.tensor_copy(out=sg[1][:], in_=xs[:, 1, :].indirect(offs_t[:]))
+        lnobs_u = keep.tile([P, PACK, S], F32, name="lnobs_u")
+        for t in range(PACK):
+            nc.vector.tensor_scalar_mul(out=lnobs_u[:, t, :], in0=lnobs[:, t, :], scalar1=unit_t[:, t : t + 1])
+        nc.vector.tensor_copy(out=xg[1][:], in_=xw[1][:].bitcast(U32).indirect(offs_t[:]))
+        deal_words(2)
+        deal_words(3)
+        dl = [psum.tile([P, S], F32, name="dl%d" % t, tag="dl%d" % t) for t in range(PACK)]
         mu = [psum.tile([P, S], F32, name="mu%d" % t, tag="bank%d" % t) for t in range(PACK)]
 
         def first_products(t, o):
-            for w, acc in ((1, mu[t]), (0, dl[t])):
+            for w, acc in (((0, dl[t]), (1, mu[t])) if o == 0 else ((1, mu[t]), (0, dl[t]))):
                 nc.tensor.matmul_mx(
                     out=acc[:],
-                    lhsT=wd[t][:, PASSES * w + o, :].bitcast(FP4X4),
-                    lhsT_scale=wsd[w][t][:, o, :],
+                    lhsT=wd[t // 2][:, PASSES * w + o, t % 2, :].bitcast(FP4X4),
+                    lhsT_scale=wsd[w][:, o, P * t : P * (t + 1)],
                     rhs=xg[o][:].bitcast(FP8X4),
                     rhs_scale=sg[o][:],
                     start=(o == 0),
@@ -124,18 +142,18 @@ def tile_picked_yblpsh_crs_p_kernel(
         tm = tiles("tm", [P, S], F32, PACK)
         td = tiles("td", [P, S], F32, PACK)
         taste = tiles("taste", [P, S], F32, PACK)
-        util = tiles("util", [P, S], F32, PACK)
-        eu = keep.tile([P, PACK, S], F32, name="eu", tag="eu_then_lnobs")
+        util = keep.tile([P, PACK, S], F32, name="util")
+        eu = keep.tile([P, PACK, S], F32, name="eu")
         mkt = keep.tile([P, PACK, V], F32, name="mkt")
 
         def utility(t):
             nc.scalar.activation(out=tm[t][:], in_=mu[t][:], func=ACT.Tanh)
             nc.scalar.activation(out=td[t][:], in_=dl[t][:], func=ACT.Tanh)
             nc.vector.tensor_tensor(out=taste[t][:], in0=tm[t][:], in1=nu_t[:, t, :], op=ALU.mult)
-            nc.vector.tensor_tensor(out=util[t][:], in0=taste[t][:], in1=td[t][:], op=ALU.add)
+            nc.vector.tensor_tensor(out=util[:, t, :], in0=taste[t][:], in1=td[t][:], op=ALU.add)
 
         def market(t):
-            nc.scalar.activation(out=eu[:, t, :], in_=util[t][:], func=ACT.Exp, scale=0.9)
+            nc.scalar.activation(out=eu[:, t, :], in_=util[:, t, :], func=ACT.Exp, scale=0.9)
             nc.vector.tensor_reduce(out=mkt[:, t, :], in_=eu[:, t, :].rearrange("p (v d) -> p v d", d=D), axis=AX.X, op=ALU.add)
 
         utility(0)
@@ -144,93 +162,103 @@ def tile_picked_yblpsh_crs_p_kernel(
             market(t - 1)
         market(PACK - 1)
 
-        lnden = keep.tile([P, PACK, V], F32, name="lnden")
-        lnobs = keep.tile([P, PACK, S], F32, name="lnobs", tag="eu_then_lnobs")
-        nc.scalar.activation(out=lnden[:], in_=mkt[:], func=ACT.Ln, bias=1.0)
-        for h in range(2):
-            nc.scalar.activation(out=lnobs[:, 2 * h : 2 * h + 2, :], in_=obs_t[:, 2 * h : 2 * h + 2, :], func=ACT.Ln)
-
-        lnshr = tiles("lnshr", [P, S], F32, PACK)
-        gap = tiles("gap", [P, S], F32, PACK)
-        dnew = tiles("dnew", [P, S], F32, PACK)
-        shr = tiles("shr", [P, S], F32, PACK)
-        rival = tiles("rival", [P, S], F32, PACK)
-        both = tiles("both", [P, S], F32, PACK)
-        cut = tiles("cut", [P, S], F32, PACK)
-        hid = tiles("hid", [P, PACK, HALF], BF16, 2)
-
-        def log_share(t):
+        base = keep.tile([P, PACK, S], F32, name="base")
+        for t in range(PACK):
             nc.vector.scalar_tensor_tensor(
-                out=lnshr[t][:].rearrange("p (v d) -> p v d", d=D),
-                in0=util[t][:].rearrange("p (v d) -> p v d", d=D),
+                out=base[:, t, :], in0=dl[t][:], scalar=unit_t[:, t : t + 1], in1=lnobs_u[:, t, :], op0=ALU.mult, op1=ALU.add
+            )
+
+        lnden = keep.tile([P, PACK, V], F32, name="lnden")
+        nc.scalar.activation(out=lnden[:], in_=mkt[:], func=ACT.Ln, bias=1.0)
+        lnshr = keep.tile([P, PACK, S], F32, name="lnshr")
+        minus_unit = keep.tile([P, PACK], F32, name="minus_unit")
+        dnew = keep.tile([P, PACK, S], F32, name="dnew")
+        shr = tiles("shr", [P, S], F32, PACK)
+        rival = keep.tile([P, PACK, S], F32, name="rival")
+        both = keep.tile([P, PACK, S], F32, name="both")
+        cut = keep.tile([P, PACK, S], F32, name="cut")
+
+        nc.vector.tensor_scalar_mul(out=minus_unit[:], in0=unit_t[:], scalar1=-1.0)
+        for pair in range(2):
+            rows = slice(2 * pair, 2 * pair + 2)
+            nc.vector.scalar_tensor_tensor(
+                out=lnshr[:, rows, :].rearrange("p t (v d) -> p (t v) d", d=D),
+                in0=util[:, rows, :].rearrange("p t (v d) -> p (t v) d", d=D),
                 scalar=0.9,
-                in1=lnden[:, t, :].unsqueeze(2).to_broadcast([P, V, D]),
+                in1=lnden[:, rows, :].rearrange("p t v -> p (t v)").unsqueeze(2).to_broadcast([P, 2 * V, D]),
                 op0=ALU.mult,
                 op1=ALU.subtract,
             )
-
-        def minus_log_share(t):
-            nc.vector.tensor_tensor(out=gap[t][:], in0=dl[t][:], in1=lnshr[t][:], op=ALU.subtract)
-
-        log_share(0)
-        for t in range(1, PACK):
-            log_share(t)
-            minus_log_share(t - 1)
-        minus_log_share(PACK - 1)
         for t in range(PACK):
-            nc.vector.tensor_tensor(out=dnew[t][:], in0=gap[t][:], in1=lnobs[:, t, :], op=ALU.add)
-        for t in range(PACK):
-            nc.scalar.activation(out=shr[t][:], in_=lnshr[t][:], func=ACT.Exp)
-            for h in range(2):
-                nc.scalar.activation(
-                    out=rival[t][:, h * HALF : (h + 1) * HALF],
-                    in_=shr[t][:].indirect(riv_t[:, h * (HALF // 16) : (h + 1) * (HALF // 16)]),
-                    func=ACT.Copy,
-                )
-
-        def step(kind, t, h):
-            cols = slice(h * HALF, (h + 1) * HALF)
-            u = unit_t[:, t : t + 1]
-            if kind == 0:
-                nc.vector.tensor_tensor(out=both[t][:, cols], in0=rival[t][:, cols], in1=dnew[t][:, cols], op=ALU.add)
-            elif kind == 1:
-                nc.vector.scalar_tensor_tensor(
-                    out=cut[t][:, cols], in0=both[t][:, cols], scalar=u, in1=shr[t][:, cols], op0=ALU.mult, op1=ALU.mult
-                )
-            else:
-                nc.vector.scalar_tensor_tensor(
-                    out=hid[h][:, t, :], in0=dnew[t][:, cols], scalar=u, in1=cut[t][:, cols], op0=ALU.mult, op1=ALU.subtract
-                )
-
-        for t in range(PACK):
-            for kind in range(3):
-                for h in range(2):
-                    step(kind, t, h)
-
-        woven = tiles("woven", [P, HALF, PACK], BF16, 2)
-        codes = tiles("codes", [P, HALF], U32, 2)
-        plane = tiles("plane", [P, HALF], U8, 2)
-        res = tiles("res", [P, HALF], F32, 4)
-        for h in range(2):
-            nc.vector.tensor_copy(
-                out=woven[h][:].rearrange("p (c i) t -> p c t i", i=4), in_=hid[h][:].rearrange("p t (c i) -> p c t i", i=4)
+            nc.vector.scalar_tensor_tensor(
+                out=dnew[:, t, :], in0=lnshr[:, t, :], scalar=minus_unit[:, t : t + 1], in1=base[:, t, :], op0=ALU.mult, op1=ALU.add
             )
-        for h in range(2):
-            nc.vector.quantize_mx(out=codes[h][:].bitcast(FP8X4), scales=plane[h][:], in_=woven[h][:].rearrange("p j t -> p (j t)"))
-        for h in range(2):
+
+        def fetch(t, h):
+            nc.scalar.activation(
+                out=rival[:, t, h * HALF : (h + 1) * HALF],
+                in_=shr[t][:].indirect(riv_t[:, h * (HALF // 16) : (h + 1) * (HALF // 16)]),
+                func=ACT.Copy,
+            )
+
+        for t in range(PACK):
+            nc.scalar.activation(out=shr[t][:], in_=lnshr[:, t, :], func=ACT.Exp)
+            fetch(t, 0)
+        for t in range(PACK):
+            fetch(t, 1)
+
+        chunks = [(0, HALF), (HALF, HALF // 2), (HALF + HALF // 2, HALF // 2)]
+        woven = [keep.tile([P, width, PACK], BF16, name="woven%d" % c, align_bytes=64) for c, (first, width) in enumerate(chunks)]
+        codes = [keep.tile([P, width], U32, name="codes%d" % c, align_bytes=64) for c, (first, width) in enumerate(chunks)]
+        plane = [keep.tile([P, width], U8, name="plane%d" % c, align_bytes=64) for c, (first, width) in enumerate(chunks)]
+
+        def combine(h):
+            cols = slice(h * HALF, (h + 1) * HALF)
+            for pair in range(2):
+                for t in (2 * pair, 2 * pair + 1):
+                    nc.vector.scalar_tensor_tensor(
+                        out=both[:, t, cols], in0=rival[:, t, cols], scalar=unit_t[:, t : t + 1], in1=dnew[:, t, cols],
+                        op0=ALU.mult, op1=ALU.add,
+                    )
+                for t in (2 * pair, 2 * pair + 1):
+                    nc.vector.tensor_tensor(out=cut[:, t, cols], in0=both[:, t, cols], in1=shr[t][:, cols], op=ALU.mult)
+
+        def weave(c):
+            first, width = chunks[c]
+            nc.vector.tensor_tensor(
+                out=woven[c][:].rearrange("p (c i) t -> p c t i", i=4),
+                in0=dnew[:, :, first : first + width].rearrange("p t (c i) -> p c t i", i=4),
+                in1=cut[:, :, first : first + width].rearrange("p t (c i) -> p c t i", i=4),
+                op=ALU.subtract,
+            )
+
+        def finish(c):
+            first, width = chunks[c]
+            nc.vector.quantize_mx(out=codes[c][:].bitcast(FP8X4), scales=plane[c][:], in_=woven[c][:].rearrange("p j t -> p (j t)"))
             for m in range(N // P):
-                acc = psum.tile([P, HALF], F32, name="acc%d%d" % (h, m), tag="bank%d" % (2 * h + m))
+                bank = 2 * c + m
+                acc = psum.tile([P, width], F32, name="acc%d" % bank, tag=("bank%d" % bank if bank < PACK else "dl%d" % (bank - PACK)))
+                res = keep.tile([P, width], F32, name="res%d" % bank)
                 nc.tensor.matmul_mx(
                     out=acc[:],
                     lhsT=w3w[:, 2 * P * m : 2 * P * (m + 1)].bitcast(FP4X4),
                     lhsT_scale=w3s[:, 0, P * m : P * (m + 1)],
-                    rhs=codes[h][:].bitcast(FP8X4),
-                    rhs_scale=plane[h][:],
+                    rhs=codes[c][:].bitcast(FP8X4),
+                    rhs_scale=plane[c][:],
                     start=True,
                     stop=True,
                 )
-                if m == 0:
-                    nc.scalar.copy(out=res[2 * h + m][:], in_=acc[:])
+                if m == 0 or c < 2:
+                    nc.scalar.copy(out=res[:], in_=acc[:])
                 else:
-                    nc.vector.tensor_copy(out=res[2 * h + m][:], in_=acc[:])
-                nc.sync.dma_start(out=out[P * m : P * (m + 1), h * HALF : (h + 1) * HALF], in_=res[2 * h + m][:])
+                    nc.vector.tensor_copy(out=res[:], in_=acc[:])
+                nc.sync.dma_start(out=out[P * m : P * (m + 1), first : first + width], in_=res[:])
+
+        combine(0)
+        weave(0)
+        combine(1)
+        finish(0)
+        weave(1)
+        weave(2)
+        finish(1)
+        finish(2)

@@ -72,7 +72,6 @@ def tile_picked_yblpsh_crs_p_kernel(
             load_plane_rows(nc.sync, ws[0], w1_scales, q)
         for q in range(4):
             load_plane_rows(nc.sync if q < 1 else nc.gpsimd, ws[1], w2_scales, q)
-        nc.gpsimd.dma_start(out=unit_t[:], in_=unit.rearrange("(p t) o -> p (t o)", t=PACK))
         obs_rows = obs.rearrange("(p t) j -> p t j", t=PACK)
         for h in range(2):
             nc.sync.dma_start(out=obs_t[:, 2 * h : 2 * h + 2, :], in_=obs_rows[:, 2 * h : 2 * h + 2, :])
@@ -80,6 +79,7 @@ def tile_picked_yblpsh_crs_p_kernel(
         nu_rows = nu.rearrange("(p t) j -> p t j", t=PACK)
         for h in range(2):
             nc.sync.dma_start(out=nu_t[:, 2 * h : 2 * h + 2, :], in_=nu_rows[:, 2 * h : 2 * h + 2, :])
+        nc.sync.dma_start(out=unit_t[:], in_=unit.rearrange("(p t) o -> p (t o)", t=PACK))
         nc.sync.dma_start(riv_t[:], riv)
         nc.sync.dma_start(out=w3w[:].bitcast(I32), in_=w3_words[0].bitcast(I32))
         for q in range(4):
@@ -171,27 +171,25 @@ def tile_picked_yblpsh_crs_p_kernel(
         lnden = keep.tile([P, PACK, V], F32, name="lnden")
         nc.scalar.activation(out=lnden[:], in_=mkt[:], func=ACT.Ln, bias=1.0)
         lnshr = keep.tile([P, PACK, S], F32, name="lnshr")
-        minus_unit = keep.tile([P, PACK], F32, name="minus_unit")
         dnew = keep.tile([P, PACK, S], F32, name="dnew")
         shr = tiles("shr", [P, S], F32, PACK)
         rival = keep.tile([P, PACK, S], F32, name="rival")
         both = keep.tile([P, PACK, S], F32, name="both")
         cut = keep.tile([P, PACK, S], F32, name="cut")
 
-        nc.vector.tensor_scalar_mul(out=minus_unit[:], in0=unit_t[:], scalar1=-1.0)
         for pair in range(2):
             rows = slice(2 * pair, 2 * pair + 2)
             nc.vector.scalar_tensor_tensor(
                 out=lnshr[:, rows, :].rearrange("p t (v d) -> p (t v) d", d=D),
                 in0=util[:, rows, :].rearrange("p t (v d) -> p (t v) d", d=D),
-                scalar=0.9,
+                scalar=-0.9,
                 in1=lnden[:, rows, :].rearrange("p t v -> p (t v)").unsqueeze(2).to_broadcast([P, 2 * V, D]),
                 op0=ALU.mult,
-                op1=ALU.subtract,
+                op1=ALU.add,
             )
         for t in range(PACK):
             nc.vector.scalar_tensor_tensor(
-                out=dnew[:, t, :], in0=lnshr[:, t, :], scalar=minus_unit[:, t : t + 1], in1=base[:, t, :], op0=ALU.mult, op1=ALU.add
+                out=dnew[:, t, :], in0=lnshr[:, t, :], scalar=unit_t[:, t : t + 1], in1=base[:, t, :], op0=ALU.mult, op1=ALU.add
             )
 
         def fetch(t, h):
@@ -202,7 +200,7 @@ def tile_picked_yblpsh_crs_p_kernel(
             )
 
         for t in range(PACK):
-            nc.scalar.activation(out=shr[t][:], in_=lnshr[:, t, :], func=ACT.Exp)
+            nc.scalar.activation(out=shr[t][:], in_=lnshr[:, t, :], func=ACT.Exp, scale=-1.0)
             fetch(t, 0)
         for t in range(PACK):
             fetch(t, 1)

@@ -30,73 +30,62 @@ def tile_picked_yblpsh_crs_p_kernel(
     nc = tc.nc
     with ExitStack() as ctx:
         keep = ctx.enter_context(tc.tile_pool(name="keep", bufs=1))
+        reuse = ctx.enter_context(tc.tile_pool(name="reuse", bufs=1))
         psum = ctx.enter_context(tc.psum_pool(name="psum", bufs=1))
 
         def tiles(name, shape, dtype, count):
             return [keep.tile(shape, dtype, name=name + str(i), tag=name + str(i), align_bytes=64) for i in range(count)]
 
-        def load_plane_rows(queue, plane, scales, quadrant):
-            queue.dma_start(
-                out=plane[32 * quadrant : 32 * quadrant + 4].bitcast(I32),
-                in_=scales[:, 4 * quadrant : 4 * quadrant + 4, :].rearrange("o r c -> r o c").bitcast(I32),
-            )
+        def load_plane_rows(queue, plane, scales, r):
+            queue.dma_start(out=plane[r:P:32].bitcast(I32), in_=scales[:, r:16:4, :].rearrange("o q c -> q o c").bitcast(I32))
 
         offs_t = keep.tile([P, S // 16], U16, name="offs_t")
         riv_t = keep.tile([P, S // 16], U16, name="riv_t")
-        xs = keep.tile([P, PASSES, T], U8, name="xs", tag="xs_then_nu", align_bytes=64)
+        xs = keep.tile([P, PASSES, T], U8, name="xs", align_bytes=64)
+        xplane = keep.tile([P, PASSES, S], U8, name="xplane", align_bytes=64)
         ws = tiles("ws", [P, PASSES, H], U8, 2)
         ww = keep.tile([P, 2 * PASSES, 2 * H], U8, name="ww", tag="ww", align_bytes=64)
-        xw = [keep.tile([P, T], I32, name="xw%d" % o, tag="xw%d" % o, align_bytes=64) for o in range(PASSES)]
+        xw = [
+            reuse.tile([P, T], I32, name="xw0", offset=0, align_bytes=64),
+            keep.tile([P, T], I32, name="xw1", tag="xw1", align_bytes=64),
+        ]
+        obs_t = keep.tile([P, PACK, S], F32, name="obs_t")
 
-        nu_t = keep.tile([P, PACK, S], F32, name="nu_t")
-        w3s = keep.tile([P, 1, N], U8, name="w3s", align_bytes=64)
-        w3w = keep.tile([P, 2 * N], U8, name="w3w", align_bytes=64)
-        unit_t = keep.tile([P, PACK], F32, name="unit_t")
         xs_words = xs[:].rearrange("p o c -> p (o c)").bitcast(I32)
         nc.gpsimd.memset(xs_words[:, 0:640], 0)
         nc.vector.memset(xs_words[:, 640:1024], 0)
         nc.vector.memset(ws[0][:].bitcast(I32), 0)
         nc.vector.memset(ws[1][:].bitcast(I32), 0)
+        nc.vector.memset(xplane[:].bitcast(I32), 0)
 
-        nc.vector.memset(w3s[:].bitcast(I32), 0)
-        obs_t = keep.tile([P, PACK, S], F32, name="obs_t", align_bytes=64)
         nc.sync.dma_start(offs_t[:], offs)
         for w, words in enumerate((w1_words, w2_words)):
             nc.sync.dma_start(
                 out=ww[:, PASSES * w : PASSES * (w + 1), :].bitcast(I32), in_=words.rearrange("o p c -> p o c").bitcast(I32)
             )
-        for q in range(4):
-            load_plane_rows(nc.sync, xs, x_scales, q)
-        nc.sync.dma_start(out=xw[0][:], in_=x_words[0].rearrange("p c r -> p (c r)").bitcast(I32))
-        for q in range(4):
-            load_plane_rows(nc.sync, ws[0], w1_scales, q)
-        for q in range(4):
-            load_plane_rows(nc.sync if q < 1 else nc.gpsimd, ws[1], w2_scales, q)
+        nc.sync.dma_start(out=xs[0:P:8].bitcast(I32), in_=x_scales.rearrange("o q c -> q o c").bitcast(I32))
         obs_rows = obs.rearrange("(p t) j -> p t j", t=PACK)
-        for h in range(2):
-            nc.sync.dma_start(out=obs_t[:, 2 * h : 2 * h + 2, :], in_=obs_rows[:, 2 * h : 2 * h + 2, :])
+        nc.sync.dma_start(out=obs_t[:, 0:1, :], in_=obs_rows[:, 0:1, :])
+        nc.sync.dma_start(out=xw[0][:], in_=x_words[0].rearrange("p c r -> p (c r)").bitcast(I32))
+        for r in range(4):
+            load_plane_rows(nc.sync, ws[0], w1_scales, r)
+            load_plane_rows(nc.gpsimd, ws[1], w2_scales, r)
+        nc.sync.dma_start(out=obs_t[:, 1:PACK, :], in_=obs_rows[:, 1:PACK, :])
         nc.sync.dma_start(out=xw[1][:], in_=x_words[1].rearrange("p c r -> p (c r)").bitcast(I32))
-        nu_rows = nu.rearrange("(p t) j -> p t j", t=PACK)
-        for h in range(2):
-            nc.sync.dma_start(out=nu_t[:, 2 * h : 2 * h + 2, :], in_=nu_rows[:, 2 * h : 2 * h + 2, :])
-        nc.sync.dma_start(out=unit_t[:], in_=unit.rearrange("(p t) o -> p (t o)", t=PACK))
         nc.sync.dma_start(riv_t[:], riv)
-        nc.sync.dma_start(out=w3w[:].bitcast(I32), in_=w3_words[0].bitcast(I32))
-        for q in range(4):
-            load_plane_rows(nc.sync, w3s, w3_scales, q)
 
         lnobs = keep.tile([P, PACK, S], F32, name="lnobs")
-        for h in range(2):
-            nc.scalar.activation(out=lnobs[:, 2 * h : 2 * h + 2, :], in_=obs_t[:, 2 * h : 2 * h + 2, :], func=ACT.Ln)
+        for rows in (slice(0, 1), slice(1, PACK)):
+            nc.scalar.activation(out=lnobs[:, rows, :], in_=obs_t[:, rows, :], func=ACT.Ln)
 
-        wd = [
-            keep.tile([P, 2 * PASSES, 2, 2 * P], U8, name="wd%d" % h, tag=tag, align_bytes=64) for h, tag in enumerate(("wd0", "xw1"))
+        wd = tiles("wd", [P, 2 * PASSES, 2 * P], U8, PACK)
+        wsd = [
+            reuse.tile([P, PASSES, H], U8, name="wsd%d" % w, offset=4096 + 1024 * w, align_bytes=64) for w in range(2)
         ]
-        wsd = tiles("wsd", [P, PASSES, H], U8, 2)
 
         def deal_words(t):
             nc.vector.tensor_copy(
-                out=wd[t // 2][:, :, t % 2, :].rearrange("p a (m b) -> p a m b", b=2),
+                out=wd[t][:].rearrange("p a (m b) -> p a m b", b=2),
                 in_=ww[:].rearrange("p a (m t b) -> p a m t b", t=PACK, b=2)[:, :, :, t, :],
             )
 
@@ -105,39 +94,60 @@ def tile_picked_yblpsh_crs_p_kernel(
                 out=wsd[w][:].rearrange("p o (t m) -> p o t m", t=PACK), in_=ws[w][:].rearrange("p o (m t) -> p o t m", t=PACK)
             )
 
-        xg = [keep.tile([P, S], U32, name="xg%d" % o, tag=tag, align_bytes=64) for o, tag in enumerate(("xg0", "ws1"))]
-        sg = tiles("sg", [P, S], U8, PASSES)
+        xg = tiles("xg", [P, S], U32, PASSES)
+        sg = keep.tile([P, PASSES, S], U8, name="sg", align_bytes=64)
+        for o in range(PASSES):
+            nc.vector.tensor_copy(out=sg[:, o, :], in_=xs[:, o, :].indirect(offs_t[:]))
+        for r in range(4):
+            nc.scalar.dma_start(out=xplane[r:P:32].bitcast(I32), in_=sg[8 * r : P : 32].bitcast(I32))
         deal_words(0)
         deal_words(1)
-        nc.vector.tensor_copy(out=sg[0][:], in_=xs[:, 0, :].indirect(offs_t[:]))
         nc.vector.tensor_copy(out=xg[0][:], in_=xw[0][:].bitcast(U32).indirect(offs_t[:]))
         deal_scales(0)
         deal_scales(1)
-        nc.vector.tensor_copy(out=sg[1][:], in_=xs[:, 1, :].indirect(offs_t[:]))
-        lnobs_u = keep.tile([P, PACK, S], F32, name="lnobs_u")
-        for t in range(PACK):
-            nc.vector.tensor_scalar_mul(out=lnobs_u[:, t, :], in0=lnobs[:, t, :], scalar1=unit_t[:, t : t + 1])
-        nc.vector.tensor_copy(out=xg[1][:], in_=xw[1][:].bitcast(U32).indirect(offs_t[:]))
         deal_words(2)
         deal_words(3)
-        dl = [psum.tile([P, S], F32, name="dl%d" % t, tag="dl%d" % t) for t in range(PACK)]
-        mu = [psum.tile([P, S], F32, name="mu%d" % t, tag="bank%d" % t) for t in range(PACK)]
+        nc.vector.tensor_copy(out=xg[1][:], in_=xw[1][:].bitcast(U32).indirect(offs_t[:]))
 
-        def first_products(t, o):
-            for w, acc in (((0, dl[t]), (1, mu[t])) if o == 0 else ((1, mu[t]), (0, dl[t]))):
-                nc.tensor.matmul_mx(
-                    out=acc[:],
-                    lhsT=wd[t // 2][:, PASSES * w + o, t % 2, :].bitcast(FP4X4),
-                    lhsT_scale=wsd[w][:, o, P * t : P * (t + 1)],
-                    rhs=xg[o][:].bitcast(FP8X4),
-                    rhs_scale=sg[o][:],
-                    start=(o == 0),
-                    stop=(o == PASSES - 1),
-                )
+        unit_t = reuse.tile([P, PACK], F32, name="unit_t", offset=6144, align_bytes=64)
+        nu_t = [
+            reuse.tile([P, 2, S], F32, name="nu0", offset=0, align_bytes=64),
+            keep.tile([P, 2, S], F32, name="nu1", tag="ws1", align_bytes=64),
+        ]
+        nc.sync.dma_start(out=unit_t[:], in_=unit.rearrange("(p t) o -> p (t o)", t=PACK))
+        nu_rows = nu.rearrange("(p t) j -> p t j", t=PACK)
+        for h in range(2):
+            nc.sync.dma_start(out=nu_t[h][:], in_=nu_rows[:, 2 * h : 2 * h + 2, :])
+        w3w = keep.tile([P, 2 * N], U8, name="w3w", tag="ww", align_bytes=64)
+        w3s = keep.tile([P, 1, N], U8, name="w3s", tag="ws0", align_bytes=64)
+        nc.vector.memset(w3s[:].bitcast(I32), 0)
+        nc.sync.dma_start(out=w3w[:].bitcast(I32), in_=w3_words[0].bitcast(I32))
+        for r in range(4):
+            load_plane_rows(nc.sync, w3s, w3_scales, r)
 
-        for o in range(PASSES):
-            for t in range(PACK):
-                first_products(t, o)
+        lnobs_u = keep.tile([P, PACK, S], F32, name="lnobs_u", tag="xw1", align_bytes=64)
+        for t in range(PACK):
+            nc.vector.tensor_scalar_mul(out=lnobs_u[:, t, :], in0=lnobs[:, t, :], scalar1=unit_t[:, t : t + 1])
+
+        mu_banks = ("bank0", "bank1", "bank0", "bank0")
+        dl_banks = ("bank2", "bank3", "bank1", "bank4")
+        dl = []
+        mu = []
+
+        def first_products(t):
+            mu.append(psum.tile([P, S], F32, name="mu%d" % t, tag=mu_banks[t]))
+            dl.append(psum.tile([P, S], F32, name="dl%d" % t, tag=dl_banks[t]))
+            for w, acc in ((1, mu[t]), (0, dl[t])):
+                for o in range(PASSES):
+                    nc.tensor.matmul_mx(
+                        out=acc[:],
+                        lhsT=wd[t][:, PASSES * w + o, :].bitcast(FP4X4),
+                        lhsT_scale=wsd[w][:, o, P * t : P * (t + 1)],
+                        rhs=xg[o][:].bitcast(FP8X4),
+                        rhs_scale=xplane[:, o, :],
+                        start=(o == 0),
+                        stop=(o == PASSES - 1),
+                    )
 
         tm = tiles("tm", [P, S], F32, PACK)
         td = tiles("td", [P, S], F32, PACK)
@@ -147,9 +157,10 @@ def tile_picked_yblpsh_crs_p_kernel(
         mkt = keep.tile([P, PACK, V], F32, name="mkt")
 
         def utility(t):
+            first_products(t)
             nc.scalar.activation(out=tm[t][:], in_=mu[t][:], func=ACT.Tanh)
             nc.scalar.activation(out=td[t][:], in_=dl[t][:], func=ACT.Tanh)
-            nc.vector.tensor_tensor(out=taste[t][:], in0=tm[t][:], in1=nu_t[:, t, :], op=ALU.mult)
+            nc.vector.tensor_tensor(out=taste[t][:], in0=tm[t][:], in1=nu_t[t // 2][:, t % 2, :], op=ALU.mult)
             nc.vector.tensor_tensor(out=util[:, t, :], in0=taste[t][:], in1=td[t][:], op=ALU.add)
 
         def market(t):
@@ -235,7 +246,7 @@ def tile_picked_yblpsh_crs_p_kernel(
             nc.vector.quantize_mx(out=codes[c][:].bitcast(FP8X4), scales=plane[c][:], in_=woven[c][:].rearrange("p j t -> p (j t)"))
             for m in range(N // P):
                 bank = 2 * c + m
-                acc = psum.tile([P, width], F32, name="acc%d" % bank, tag=("bank%d" % bank if bank < PACK else "dl%d" % (bank - PACK)))
+                acc = psum.tile([P, width], F32, name="acc%d" % bank, tag="bank%d" % ((5, 6, 7, 0, 2, 3)[bank]))
                 res = keep.tile([P, width], F32, name="res%d" % bank)
                 nc.tensor.matmul_mx(
                     out=acc[:],

@@ -79,9 +79,7 @@ def tile_picked_yblpsh_crs_p_kernel(
             nc.scalar.activation(out=lnobs[:, rows, :], in_=obs_t[:, rows, :], func=ACT.Ln)
 
         wd = tiles("wd", [P, 2 * PASSES, 2 * P], U8, PACK)
-        wsd = [
-            reuse.tile([P, PASSES, H], U8, name="wsd%d" % w, offset=4096 + 1024 * w, align_bytes=64) for w in range(2)
-        ]
+        wsd = tiles("wsd", [P, PASSES, H], U8, 2)
 
         def deal_words(t):
             nc.vector.tensor_copy(
@@ -89,9 +87,11 @@ def tile_picked_yblpsh_crs_p_kernel(
                 in_=ww[:].rearrange("p a (m t b) -> p a m t b", t=PACK, b=2)[:, :, :, t, :],
             )
 
-        def deal_scales(w):
-            nc.vector.tensor_copy(
-                out=wsd[w][:].rearrange("p o (t m) -> p o t m", t=PACK), in_=ws[w][:].rearrange("p o (m t) -> p o t m", t=PACK)
+        def deal_scales(w, pair):
+            rows = slice(2 * pair, 2 * pair + 2)
+            nc.gpsimd.tensor_copy(
+                out=wsd[w][:].rearrange("p o (t m) -> p o t m", t=PACK)[:, :, rows, :],
+                in_=ws[w][:].rearrange("p o (m t) -> p o t m", t=PACK)[:, :, rows, :],
             )
 
         xg = tiles("xg", [P, S], U32, PASSES)
@@ -103,8 +103,9 @@ def tile_picked_yblpsh_crs_p_kernel(
         deal_words(0)
         deal_words(1)
         nc.vector.tensor_copy(out=xg[0][:], in_=xw[0][:].bitcast(U32).indirect(offs_t[:]))
-        deal_scales(0)
-        deal_scales(1)
+        for pair in range(2):
+            deal_scales(1, pair)
+            deal_scales(0, pair)
         deal_words(2)
         deal_words(3)
         nc.vector.tensor_copy(out=xg[1][:], in_=xw[1][:].bitcast(U32).indirect(offs_t[:]))
@@ -120,7 +121,7 @@ def tile_picked_yblpsh_crs_p_kernel(
             nc.sync.dma_start(out=nu_t[h][:], in_=nu_rows[:, 2 * h : 2 * h + 2, :])
         w3w = keep.tile([P, 2 * N], U8, name="w3w", tag="ww", align_bytes=64)
         w3s = keep.tile([P, 1, N], U8, name="w3s", tag="ws0", align_bytes=64)
-        nc.vector.memset(w3s[:].bitcast(I32), 0)
+        nc.gpsimd.memset(w3s[:].bitcast(I32), 0)
         nc.sync.dma_start(out=w3w[:].bitcast(I32), in_=w3_words[0].bitcast(I32))
         for r in range(4):
             load_plane_rows(nc.sync, w3s, w3_scales, r)

from contextlib import ExitStack

import concourse.mybir as mybir

K, T, S, D, N, H = 1024, 2048, 512, 4, 256, 512
FLOPS = 2 * (2 * K * H * S + H * N * S)

F32 = mybir.dt.float32
BF16 = mybir.dt.bfloat16
I32 = mybir.dt.int32
U32 = mybir.dt.uint32
U16 = mybir.dt.uint16
U8 = mybir.dt.uint8
FP8X4 = mybir.dt.float8_e4m3fn_x4
FP4X4 = mybir.dt.float4_e2m1fn_x4
ALU = mybir.AluOpType
ACT = mybir.ActivationFunctionType
AX = mybir.AxisListType

P = 128
PACK = 4
PASSES = K // (P * PACK)
V = S // D
HALF = S // 2


def tile_picked_yblpsh_crs_p_kernel(
    tc, x_words, x_scales, w1_words, w1_scales, w2_words, w2_scales, nu, obs, unit, w3_words, w3_scales, offs, riv, out
):
    nc = tc.nc
    with ExitStack() as ctx:
        keep = ctx.enter_context(tc.tile_pool(name="keep", bufs=1))
        reuse = ctx.enter_context(tc.tile_pool(name="reuse", bufs=1))
        psum = ctx.enter_context(tc.psum_pool(name="psum", bufs=1))

        def tiles(name, shape, dtype, count):
            return [keep.tile(shape, dtype, name=name + str(i), tag=name + str(i), align_bytes=64) for i in range(count)]

        def load_plane_rows(queue, plane, scales, r):
            queue.dma_start(out=plane[r:P:32].bitcast(I32), in_=scales[:, r:16:4, :].rearrange("o q c -> q o c").bitcast(I32))

        offs_t = keep.tile([P, S // 16], U16, name="offs_t")
        riv_t = keep.tile([P, S // 16], U16, name="riv_t")
        xs = keep.tile([P, PASSES, T], U8, name="xs", align_bytes=64)
        xplane = keep.tile([P, PASSES, S], U8, name="xplane", align_bytes=64)
        ws = tiles("ws", [P, PASSES, H], U8, 2)
        ww = keep.tile([P, 2 * PASSES, 2 * H], U8, name="ww", tag="ww", align_bytes=64)
        xw = [
            reuse.tile([P, T], I32, name="xw0", offset=0, align_bytes=64),
            keep.tile([P, T], I32, name="xw1", tag="xw1", align_bytes=64),
        ]
        obs_t = keep.tile([P, PACK, S], F32, name="obs_t")

        xs_words = xs[:].rearrange("p o c -> p (o c)").bitcast(I32)
        nc.gpsimd.memset(xs_words[:, 0:640], 0)
        nc.vector.memset(xs_words[:, 640:1024], 0)
        nc.vector.memset(ws[0][:].bitcast(I32), 0)
        nc.vector.memset(ws[1][:].bitcast(I32), 0)
        nc.vector.memset(xplane[:].bitcast(I32), 0)

        nc.sync.dma_start(offs_t[:], offs)
        for w, words in enumerate((w1_words, w2_words)):
            nc.sync.dma_start(
                out=ww[:, PASSES * w : PASSES * (w + 1), :].bitcast(I32), in_=words.rearrange("o p c -> p o c").bitcast(I32)
            )
        nc.sync.dma_start(out=xs[0:P:8].bitcast(I32), in_=x_scales.rearrange("o q c -> q o c").bitcast(I32))
        obs_rows = obs.rearrange("(p t) j -> p t j", t=PACK)
        nc.sync.dma_start(out=obs_t[:, 0:1, :], in_=obs_rows[:, 0:1, :])
        nc.sync.dma_start(out=xw[0][:], in_=x_words[0].rearrange("p c r -> p (c r)").bitcast(I32))
        for r in range(4):
            load_plane_rows(nc.sync, ws[0], w1_scales, r)
            load_plane_rows(nc.gpsimd, ws[1], w2_scales, r)
        nc.sync.dma_start(out=obs_t[:, 1:PACK, :], in_=obs_rows[:, 1:PACK, :])
        nc.sync.dma_start(out=xw[1][:], in_=x_words[1].rearrange("p c r -> p (c r)").bitcast(I32))
        nc.sync.dma_start(riv_t[:], riv)

        lnobs = keep.tile([P, PACK, S], F32, name="lnobs")
        for rows in (slice(0, 1), slice(1, PACK)):
            nc.scalar.activation(out=lnobs[:, rows, :], in_=obs_t[:, rows, :], func=ACT.Ln)

        wd = tiles("wd", [P, 2 * PASSES, 2 * P], U8, PACK)
        wsd = tiles("wsd", [P, PASSES, H], U8, 2)

        def deal_words(t):
            nc.vector.tensor_copy(
                out=wd[t][:].rearrange("p a (m b) -> p a m b", b=2),
                in_=ww[:].rearrange("p a (m t b) -> p a m t b", t=PACK, b=2)[:, :, :, t, :],
            )

        def deal_scales(w, pair):
            rows = slice(2 * pair, 2 * pair + 2)
            nc.gpsimd.tensor_copy(
                out=wsd[w][:].rearrange("p o (t m) -> p o t m", t=PACK)[:, :, rows, :],
                in_=ws[w][:].rearrange("p o (m t) -> p o t m", t=PACK)[:, :, rows, :],
            )

        xg = tiles("xg", [P, S], U32, PASSES)
        sg = keep.tile([P, PASSES, S], U8, name="sg", align_bytes=64)
        for o in range(PASSES):
            nc.vector.tensor_copy(out=sg[:, o, :], in_=xs[:, o, :].indirect(offs_t[:]))
        for r in range(4):
            nc.scalar.dma_start(out=xplane[r:P:32].bitcast(I32), in_=sg[8 * r : P : 32].bitcast(I32))
        deal_words(0)
        deal_words(1)
        nc.vector.tensor_copy(out=xg[0][:], in_=xw[0][:].bitcast(U32).indirect(offs_t[:]))
        for pair in range(2):
            deal_scales(1, pair)
            deal_scales(0, pair)
        deal_words(2)
        deal_words(3)
        nc.vector.tensor_copy(out=xg[1][:], in_=xw[1][:].bitcast(U32).indirect(offs_t[:]))

        unit_t = reuse.tile([P, PACK], F32, name="unit_t", offset=6144, align_bytes=64)
        nu_t = [
            reuse.tile([P, 2, S], F32, name="nu0", offset=0, align_bytes=64),
            keep.tile([P, 2, S], F32, name="nu1", tag="ws1", align_bytes=64),
        ]
        nc.sync.dma_start(out=unit_t[:], in_=unit.rearrange("(p t) o -> p (t o)", t=PACK))
        nu_rows = nu.rearrange("(p t) j -> p t j", t=PACK)
        for h in range(2):
            nc.sync.dma_start(out=nu_t[h][:], in_=nu_rows[:, 2 * h : 2 * h + 2, :])
        w3w = keep.tile([P, 2 * N], U8, name="w3w", tag="ww", align_bytes=64)
        w3s = keep.tile([P, 1, N], U8, name="w3s", tag="ws0", align_bytes=64)
        nc.gpsimd.memset(w3s[:].bitcast(I32), 0)
        nc.sync.dma_start(out=w3w[:].bitcast(I32), in_=w3_words[0].bitcast(I32))
        for r in range(4):
            load_plane_rows(nc.sync, w3s, w3_scales, r)

        lnobs_u = keep.tile([P, PACK, S], F32, name="lnobs_u", tag="xw1", align_bytes=64)
        for t in range(PACK):
            nc.vector.tensor_scalar_mul(out=lnobs_u[:, t, :], in0=lnobs[:, t, :], scalar1=unit_t[:, t : t + 1])

        mu_banks = ("bank0", "bank1", "bank0", "bank0")
        dl_banks = ("bank2", "bank3", "bank1", "bank4")
        dl = []
        mu = []

        def first_products(t):
            mu.append(psum.tile([P, S], F32, name="mu%d" % t, tag=mu_banks[t]))
            dl.append(psum.tile([P, S], F32, name="dl%d" % t, tag=dl_banks[t]))
            for w, acc in ((1, mu[t]), (0, dl[t])):
                for o in range(PASSES):
                    nc.tensor.matmul_mx(
                        out=acc[:],
                        lhsT=wd[t][:, PASSES * w + o, :].bitcast(FP4X4),
                        lhsT_scale=wsd[w][:, o, P * t : P * (t + 1)],
                        rhs=xg[o][:].bitcast(FP8X4),
                        rhs_scale=xplane[:, o, :],
                        start=(o == 0),
                        stop=(o == PASSES - 1),
                    )

        tm = tiles("tm", [P, S], F32, PACK)
        td = tiles("td", [P, S], F32, PACK)
        taste = tiles("taste", [P, S], F32, PACK)
        util = keep.tile([P, PACK, S], F32, name="util")
        eu = keep.tile([P, PACK, S], F32, name="eu")
        mkt = keep.tile([P, PACK, V], F32, name="mkt")

        def utility(t):
            first_products(t)
            nc.scalar.activation(out=tm[t][:], in_=mu[t][:], func=ACT.Tanh)
            nc.scalar.activation(out=td[t][:], in_=dl[t][:], func=ACT.Tanh)
            nc.vector.tensor_tensor(out=taste[t][:], in0=tm[t][:], in1=nu_t[t // 2][:, t % 2, :], op=ALU.mult)
            nc.vector.tensor_tensor(out=util[:, t, :], in0=taste[t][:], in1=td[t][:], op=ALU.add)

        def market(t):
            nc.scalar.activation(out=eu[:, t, :], in_=util[:, t, :], func=ACT.Exp, scale=0.9)
            nc.vector.tensor_reduce(out=mkt[:, t, :], in_=eu[:, t, :].rearrange("p (v d) -> p v d", d=D), axis=AX.X, op=ALU.add)

        utility(0)
        for t in range(1, PACK):
            utility(t)
            market(t - 1)
        market(PACK - 1)

        base = keep.tile([P, PACK, S], F32, name="base")
        for t in range(PACK):
            nc.vector.scalar_tensor_tensor(
                out=base[:, t, :], in0=dl[t][:], scalar=unit_t[:, t : t + 1], in1=lnobs_u[:, t, :], op0=ALU.mult, op1=ALU.add
            )

        lnden = keep.tile([P, PACK, V], F32, name="lnden")
        nc.scalar.activation(out=lnden[:], in_=mkt[:], func=ACT.Ln, bias=1.0)
        lnshr = keep.tile([P, PACK, S], F32, name="lnshr")
        dnew = keep.tile([P, PACK, S], F32, name="dnew")
        shr = tiles("shr", [P, S], F32, PACK)
        rival = keep.tile([P, PACK, S], F32, name="rival")
        both = keep.tile([P, PACK, S], F32, name="both")
        cut = keep.tile([P, PACK, S], F32, name="cut")

        for pair in range(2):
            rows = slice(2 * pair, 2 * pair + 2)
            nc.vector.scalar_tensor_tensor(
                out=lnshr[:, rows, :].rearrange("p t (v d) -> p (t v) d", d=D),
                in0=util[:, rows, :].rearrange("p t (v d) -> p (t v) d", d=D),
                scalar=-0.9,
                in1=lnden[:, rows, :].rearrange("p t v -> p (t v)").unsqueeze(2).to_broadcast([P, 2 * V, D]),
                op0=ALU.mult,
                op1=ALU.add,
            )
        for t in range(PACK):
            nc.vector.scalar_tensor_tensor(
                out=dnew[:, t, :], in0=lnshr[:, t, :], scalar=unit_t[:, t : t + 1], in1=base[:, t, :], op0=ALU.mult, op1=ALU.add
            )

        def fetch(t, h):
            nc.scalar.activation(
                out=rival[:, t, h * HALF : (h + 1) * HALF],
                in_=shr[t][:].indirect(riv_t[:, h * (HALF // 16) : (h + 1) * (HALF // 16)]),
                func=ACT.Copy,
            )

        for t in range(PACK):
            nc.scalar.activation(out=shr[t][:], in_=lnshr[:, t, :], func=ACT.Exp, scale=-1.0)
            fetch(t, 0)
        for t in range(PACK):
            fetch(t, 1)

        chunks = [(0, HALF), (HALF, HALF // 2), (HALF + HALF // 2, HALF // 2)]
        woven = [keep.tile([P, width, PACK], BF16, name="woven%d" % c, align_bytes=64) for c, (first, width) in enumerate(chunks)]
        codes = [keep.tile([P, width], U32, name="codes%d" % c, align_bytes=64) for c, (first, width) in enumerate(chunks)]
        plane = [keep.tile([P, width], U8, name="plane%d" % c, align_bytes=64) for c, (first, width) in enumerate(chunks)]

        def combine(h):
            cols = slice(h * HALF, (h + 1) * HALF)
            for pair in range(2):
                for t in (2 * pair, 2 * pair + 1):
                    nc.vector.scalar_tensor_tensor(
                        out=both[:, t, cols], in0=rival[:, t, cols], scalar=unit_t[:, t : t + 1], in1=dnew[:, t, cols],
                        op0=ALU.mult, op1=ALU.add,
                    )
                for t in (2 * pair, 2 * pair + 1):
                    nc.vector.tensor_tensor(out=cut[:, t, cols], in0=both[:, t, cols], in1=shr[t][:, cols], op=ALU.mult)

        def weave(c):
            first, width = chunks[c]
            nc.vector.tensor_tensor(
                out=woven[c][:].rearrange("p (c i) t -> p c t i", i=4),
                in0=dnew[:, :, first : first + width].rearrange("p t (c i) -> p c t i", i=4),
                in1=cut[:, :, first : first + width].rearrange("p t (c i) -> p c t i", i=4),
                op=ALU.subtract,
            )

        def finish(c):
            first, width = chunks[c]
            nc.vector.quantize_mx(out=codes[c][:].bitcast(FP8X4), scales=plane[c][:], in_=woven[c][:].rearrange("p j t -> p (j t)"))
            for m in range(N // P):
                bank = 2 * c + m
                acc = psum.tile([P, width], F32, name="acc%d" % bank, tag="bank%d" % ((5, 6, 7, 0, 2, 3)[bank]))
                res = keep.tile([P, width], F32, name="res%d" % bank)
                nc.tensor.matmul_mx(
                    out=acc[:],
                    lhsT=w3w[:, 2 * P * m : 2 * P * (m + 1)].bitcast(FP4X4),
                    lhsT_scale=w3s[:, 0, P * m : P * (m + 1)],
                    rhs=codes[c][:].bitcast(FP8X4),
                    rhs_scale=plane[c][:],
                    start=True,
                    stop=True,
                )
                if m == 0 or c < 2:
                    nc.scalar.copy(out=res[:], in_=acc[:])
                else:
                    nc.vector.tensor_copy(out=res[:], in_=acc[:])
                nc.sync.dma_start(out=out[P * m : P * (m + 1), first : first + width], in_=res[:])

        combine(0)
        weave(0)
        combine(1)
        finish(0)
        weave(1)
        weave(2)
        finish(1)
        finish(2)
